import numpy as np, ml_dtypes
CORES = [1,9,17,25,129,137,145,153,257,265,273,281,385,393,401,409]
N = 16
PERM = [[0,13],[1,6],[2,9],[3,0],[4,15],[5,2],[6,11],[7,4],[8,1],[9,14],[10,7],[11,3],[12,10],[13,5],[14,12],[15,8]]
def setup_inputs(rng):
    return {"x": rng.standard_normal((N, 128, 256), dtype=np.float32).astype(ml_dtypes.bfloat16)}
def reference(x):
    y = np.empty_like(x)
    for s, d in PERM:
        y[d] = x[s]
    return {"y": y}

@@ -1,0 +1,109 @@
+import concourse.bass as bass
+
+ELEMS = 256
+GS = (1, 4)
+
+SCRATCH = {}
+SCRATCH.update({"stage%d" % n: ("dram", [n, 128, ELEMS // n], "bfloat16") for n in GS})
+SCRATCH.update({"land%d" % n: ("dram", [n, 128, ELEMS // n], "bfloat16") for n in GS})
+
+SEMAPHORES = ["loaded", "sent", "arr", "stored"]
+
+SPLIT_CABLE = False
+
+
+def world(h, c, k):
+    return h * 128 + c * 8 + k
+
+
+def route(s, d, topo):
+    hs, cs, hd, cd = topo.host(s), topo.chip(s), topo.host(d), topo.chip(d)
+    same_rack = topo.rack(hs) == topo.rack(hd)
+    same_par = cs % 2 == cd % 2
+    cabled = hs + hd == 3
+    if same_rack and same_par:
+        return [[s, d]]
+    if same_rack:
+        return [[s, world(hs, cs, r), d] for r in (2, 3, 6, 7)]
+    far = 3 - hs
+    if cabled and cd == cs ^ 1:
+        if SPLIT_CABLE:
+            return ([[s, world(far, cs, r), d] for r in (2, 6)] + [[s, world(hs, cs, r), d] for r in (2, 6)])
+        return [[s, world(far, cs, r), d] for r in (2, 3, 6, 7)]
+    assert not cabled
+    if not same_par:
+        if SPLIT_CABLE:
+            return ([[s, world(far, cs, r), d] for r in (2, 6)] + [[s, world(hs ^ 1, cd ^ 1, r), d] for r in (3, 7)])
+        return [[s, world(far, cs, r), d] for r in (2, 3, 6, 7)]
+    assert cs == cd
+    return ([[s, world(far, cs, k), d] for k in (0, 4)] + [[s, world(hs ^ 1, cs, k), d] for k in (0, 4)])
+
+
+def masks(src, dsts, topo):
+    off = [i for i, d in enumerate(dsts) if topo.mask(src, d) == 0x00FF]
+    on = [i for i, d in enumerate(dsts) if topo.mask(src, d) == 0xFFFF]
+    assert len(off) + len(on) == len(dsts)
+    out = [0] * len(dsts)
+    for grp, base, width in ((off, 0, 8), (on, 8 if off else 0, 8 if off else 16)):
+        if grp:
+            n = width // len(grp)
+            assert n * len(grp) == width
+            for j, i in enumerate(grp):
+                out[i] = ((1 << n) - 1) << (base + j * n)
+    return out
+
+
+def send(g, core, T, topo, items):
+    ms = masks(core, [it[0] for it in items], topo)
+    if len(items) == 1:
+        d, o, i = items[0]
+        rid, pid = topo.addr(d, core)
+        g.remote_dma(o, i, T.sem.arr, T.sem.sent, pid, rid, ms[0])
+    else:
+        trs = []
+        for (d, o, i), m in zip(items, ms):
+            rid, pid = topo.addr(d, core)
+            trs.append(bass.RemoteDMATransfer(dst_ids=[bass.DstId(rid=rid, pnc=pid)], dma_engine_mask=m,
+                                              remote_sem=T.sem.arr, src=i, dst=o))
+        g.remote_dma_fused(trs, local_sem=T.sem.sent)
+    return sum(bin(m).count("1") for m in ms)
+
+
+def plan(T, topo):
+    sends = {}
+    for s, d in T.tables["PERM"]:
+        paths = route(T.cores[s], T.cores[d], topo)
+        for slot, p in enumerate(paths):
+            for hop in range(len(p) - 1):
+                sends.setdefault(p[hop], []).append((len(paths), slot, p[hop + 1]))
+    return sends
+
+
+def rank_program(g, core, T, topo):
+    sends = plan(T, topo)
+    bufs = {"stage1": T.stage1, "stage4": T.stage4, "land1": T.land1, "land4": T.land4}
+    expect, g_in = 0, None
+    for c, lst in sends.items():
+        ms = masks(c, [it[2] for it in lst], topo)
+        for it, m in zip(lst, ms):
+            if it[2] == core:
+                expect += bin(m).count("1")
+                g_in = it[0]
+    mine = sends.get(core, [])
+    rank = T.rank_of(core)
+    sent = 0
+    if rank is not None:
+        n = mine[0][0]
+        st, ld = bufs["stage%d" % n], bufs["land%d" % n]
+        g.dma_start(st[:], T.x[:]).then_inc(T.sem.loaded, 16)
+        g.wait_ge(T.sem.loaded, 16)
+        sent = send(g, core, T, topo, [(nx, ld[sl], st[sl]) for n_, sl, nx in mine])
+        g.wait_ge(T.sem.arr, expect)
+        g.dma_start(T.y[:], bufs["land%d" % g_in][:]).then_inc(T.sem.stored, 16)
+        g.wait_ge(T.sem.stored, 16)
+    elif mine:
+        ld = bufs["land%d" % mine[0][0]]
+        g.wait_ge(T.sem.arr, expect)
+        sent = send(g, core, T, topo, [(nx, ld[sl], ld[sl]) for n_, sl, nx in mine])
+    if sent:
+        g.wait_ge(T.sem.sent, sent)

@@ -1,7 +1,7 @@
 import concourse.bass as bass
 
 ELEMS = 256
-GS = (1, 4)
+GS = (1, 2, 4)
 
 SCRATCH = {}
 SCRATCH.update({"stage%d" % n: ("dram", [n, 128, ELEMS // n], "bfloat16") for n in GS})
@@ -9,7 +9,9 @@ SCRATCH.update({"land%d" % n: ("dram", [n, 128, ELEMS // n], "bfloat16") for n i
 
 SEMAPHORES = ["loaded", "sent", "arr", "stored"]
 
-SPLIT_CABLE = False
+SPLIT_CABLE = True
+DIE1_IN_BUSY = ((3, 0),)
+DIE0_OUT_BUSY = ((3, 2),)
 
 
 def world(h, c, k):
@@ -22,7 +24,11 @@ def route(s, d, topo):
     same_par = cs % 2 == cd % 2
     cabled = hs + hd == 3
     if same_rack and same_par:
+        if SPLIT_CABLE and (hd, cd) in DIE1_IN_BUSY:
+            return [[s, world(hs, cs, r), d] for r in (4, 5)]
         return [[s, d]]
+    if same_rack and SPLIT_CABLE and (hs, cs ^ 1) in DIE0_OUT_BUSY:
+        return [[s, world(hs, cs, r), d] for r in (2, 3)]
     if same_rack:
         return [[s, world(hs, cs, r), d] for r in (2, 3, 6, 7)]
     far = 3 - hs
@@ -81,7 +87,8 @@ def plan(T, topo):
 
 def rank_program(g, core, T, topo):
     sends = plan(T, topo)
-    bufs = {"stage1": T.stage1, "stage4": T.stage4, "land1": T.land1, "land4": T.land4}
+    bufs = {"stage1": T.stage1, "stage2": T.stage2, "stage4": T.stage4,
+            "land1": T.land1, "land2": T.land2, "land4": T.land4}
     expect, g_in = 0, None
     for c, lst in sends.items():
         ms = masks(c, [it[2] for it in lst], topo)

@@ -9,9 +9,9 @@ SCRATCH.update({"land%d" % n: ("dram", [n, 128, ELEMS // n], "bfloat16") for n i
 
 SEMAPHORES = ["loaded", "sent", "arr", "stored"]
 
-SPLIT_CABLE = True
 DIE1_IN_BUSY = ((3, 0),)
 DIE0_OUT_BUSY = ((3, 2),)
+PORT_OWNERS = (2, 3, 6, 7)
 
 
 def world(h, c, k):
@@ -24,23 +24,19 @@ def route(s, d, topo):
     same_par = cs % 2 == cd % 2
     cabled = hs + hd == 3
     if same_rack and same_par:
-        if SPLIT_CABLE and (hd, cd) in DIE1_IN_BUSY:
+        if (hd, cd) in DIE1_IN_BUSY:
             return [[s, world(hs, cs, r), d] for r in (4, 5)]
         return [[s, d]]
-    if same_rack and SPLIT_CABLE and (hs, cs ^ 1) in DIE0_OUT_BUSY:
+    if same_rack and (hs, cs ^ 1) in DIE0_OUT_BUSY:
         return [[s, world(hs, cs, r), d] for r in (2, 3)]
     if same_rack:
-        return [[s, world(hs, cs, r), d] for r in (2, 3, 6, 7)]
+        return [[s, world(hs, cs, r), d] for r in PORT_OWNERS]
     far = 3 - hs
-    if cabled and cd == cs ^ 1:
-        if SPLIT_CABLE:
-            return ([[s, world(far, cs, r), d] for r in (2, 6)] + [[s, world(hs, cs, r), d] for r in (2, 6)])
-        return [[s, world(far, cs, r), d] for r in (2, 3, 6, 7)]
-    assert not cabled
+    if cabled:
+        assert cd == cs ^ 1
+        return ([[s, world(far, cs, r), d] for r in (2, 6)] + [[s, world(hs, cs, r), d] for r in (2, 6)])
     if not same_par:
-        if SPLIT_CABLE:
-            return ([[s, world(far, cs, r), d] for r in (2, 6)] + [[s, world(hs ^ 1, cd ^ 1, r), d] for r in (3, 7)])
-        return [[s, world(far, cs, r), d] for r in (2, 3, 6, 7)]
+        return ([[s, world(far, cs, r), d] for r in (2, 6)] + [[s, world(hs ^ 1, cd ^ 1, r), d] for r in (3, 7)])
     assert cs == cd
     return ([[s, world(far, cs, k), d] for k in (0, 4)] + [[s, world(hs ^ 1, cs, k), d] for k in (0, 4)])
 
@@ -104,13 +100,13 @@ def rank_program(g, core, T, topo):
         st, ld = bufs["stage%d" % n], bufs["land%d" % n]
         g.dma_start(st[:], T.x[:]).then_inc(T.sem.loaded, 16)
         g.wait_ge(T.sem.loaded, 16)
-        sent = send(g, core, T, topo, [(nx, ld[sl], st[sl]) for n_, sl, nx in mine])
+        sent = send(g, core, T, topo, [(it[2], ld[it[1]], st[it[1]]) for it in mine])
         g.wait_ge(T.sem.arr, expect)
         g.dma_start(T.y[:], bufs["land%d" % g_in][:]).then_inc(T.sem.stored, 16)
         g.wait_ge(T.sem.stored, 16)
     elif mine:
         ld = bufs["land%d" % mine[0][0]]
         g.wait_ge(T.sem.arr, expect)
-        sent = send(g, core, T, topo, [(nx, ld[sl], ld[sl]) for n_, sl, nx in mine])
+        sent = send(g, core, T, topo, [(it[2], ld[it[1]], ld[it[1]]) for it in mine])
     if sent:
         g.wait_ge(T.sem.sent, sent)

import concourse.bass as bass

ELEMS = 256
GS = (1, 2, 4)

SCRATCH = {}
SCRATCH.update({"stage%d" % n: ("dram", [n, 128, ELEMS // n], "bfloat16") for n in GS})
SCRATCH.update({"land%d" % n: ("dram", [n, 128, ELEMS // n], "bfloat16") for n in GS})

SEMAPHORES = ["loaded", "sent", "arr", "stored"]

DIE1_IN_BUSY = ((3, 0),)
DIE0_OUT_BUSY = ((3, 2),)
PORT_OWNERS = (2, 3, 6, 7)


def world(h, c, k):
    return h * 128 + c * 8 + k


def route(s, d, topo):
    hs, cs, hd, cd = topo.host(s), topo.chip(s), topo.host(d), topo.chip(d)
    same_rack = topo.rack(hs) == topo.rack(hd)
    same_par = cs % 2 == cd % 2
    cabled = hs + hd == 3
    if same_rack and same_par:
        if (hd, cd) in DIE1_IN_BUSY:
            return [[s, world(hs, cs, r), d] for r in (4, 5)]
        return [[s, d]]
    if same_rack and (hs, cs ^ 1) in DIE0_OUT_BUSY:
        return [[s, world(hs, cs, r), d] for r in (2, 3)]
    if same_rack:
        return [[s, world(hs, cs, r), d] for r in PORT_OWNERS]
    far = 3 - hs
    if cabled:
        assert cd == cs ^ 1
        return ([[s, world(far, cs, r), d] for r in (2, 6)] + [[s, world(hs, cs, r), d] for r in (2, 6)])
    if not same_par:
        return ([[s, world(far, cs, r), d] for r in (2, 6)] + [[s, world(hs ^ 1, cd ^ 1, r), d] for r in (3, 7)])
    assert cs == cd
    return ([[s, world(far, cs, k), d] for k in (0, 4)] + [[s, world(hs ^ 1, cs, k), d] for k in (0, 4)])


def masks(src, dsts, topo):
    off = [i for i, d in enumerate(dsts) if topo.mask(src, d) == 0x00FF]
    on = [i for i, d in enumerate(dsts) if topo.mask(src, d) == 0xFFFF]
    assert len(off) + len(on) == len(dsts)
    out = [0] * len(dsts)
    for grp, base, width in ((off, 0, 8), (on, 8 if off else 0, 8 if off else 16)):
        if grp:
            n = width // len(grp)
            assert n * len(grp) == width
            for j, i in enumerate(grp):
                out[i] = ((1 << n) - 1) << (base + j * n)
    return out


def send(g, core, T, topo, items):
    ms = masks(core, [it[0] for it in items], topo)
    if len(items) == 1:
        d, o, i = items[0]
        rid, pid = topo.addr(d, core)
        g.remote_dma(o, i, T.sem.arr, T.sem.sent, pid, rid, ms[0])
    else:
        trs = []
        for (d, o, i), m in zip(items, ms):
            rid, pid = topo.addr(d, core)
            trs.append(bass.RemoteDMATransfer(dst_ids=[bass.DstId(rid=rid, pnc=pid)], dma_engine_mask=m,
                                              remote_sem=T.sem.arr, src=i, dst=o))
        g.remote_dma_fused(trs, local_sem=T.sem.sent)
    return sum(bin(m).count("1") for m in ms)


def plan(T, topo):
    sends = {}
    for s, d in T.tables["PERM"]:
        paths = route(T.cores[s], T.cores[d], topo)
        for slot, p in enumerate(paths):
            for hop in range(len(p) - 1):
                sends.setdefault(p[hop], []).append((len(paths), slot, p[hop + 1]))
    return sends


def rank_program(g, core, T, topo):
    sends = plan(T, topo)
    bufs = {"stage1": T.stage1, "stage2": T.stage2, "stage4": T.stage4,
            "land1": T.land1, "land2": T.land2, "land4": T.land4}
    expect, g_in = 0, None
    for c, lst in sends.items():
        ms = masks(c, [it[2] for it in lst], topo)
        for it, m in zip(lst, ms):
            if it[2] == core:
                expect += bin(m).count("1")
                g_in = it[0]
    mine = sends.get(core, [])
    rank = T.rank_of(core)
    sent = 0
    if rank is not None:
        n = mine[0][0]
        st, ld = bufs["stage%d" % n], bufs["land%d" % n]
        g.dma_start(st[:], T.x[:]).then_inc(T.sem.loaded, 16)
        g.wait_ge(T.sem.loaded, 16)
        sent = send(g, core, T, topo, [(it[2], ld[it[1]], st[it[1]]) for it in mine])
        g.wait_ge(T.sem.arr, expect)
        g.dma_start(T.y[:], bufs["land%d" % g_in][:]).then_inc(T.sem.stored, 16)
        g.wait_ge(T.sem.stored, 16)
    elif mine:
        ld = bufs["land%d" % mine[0][0]]
        g.wait_ge(T.sem.arr, expect)
        sent = send(g, core, T, topo, [(it[2], ld[it[1]], ld[it[1]]) for it in mine])
    if sent:
        g.wait_ge(T.sem.sent, sent)
